import numpy as np
import ml_dtypes


def mxq(x, axis, fmt="e4m3"):
    dtype, down = {"e4m3": (ml_dtypes.float8_e4m3fn, 7), "e5m2": (ml_dtypes.float8_e5m2, 14)}[fmt]
    v = np.moveaxis(np.asarray(x, np.float32).astype(ml_dtypes.bfloat16).astype(np.float64), axis, -1)
    blocks = v.reshape(v.shape[:-1] + (-1, 32))
    amax = np.abs(blocks).max(-1, keepdims=True)
    byte = np.maximum(np.where(amax > 0, np.frexp(amax)[1] - 1 + 127, 0) - down, 1)
    scale = np.exp2(byte - 127.0)
    codes = (blocks / scale).astype(np.float32).astype(dtype).astype(np.float64)
    return np.moveaxis((codes * scale).reshape(v.shape), -1, axis)


WIDE = False


def mx_kscale(k):
    if not WIDE:
        return np.ones(k)
    levels = np.array([10, -10, 5, -5, 0])
    if k % 512:
        return np.exp2(np.random.permutation(np.resize(levels, k // 32))).repeat(32)
    a = np.empty((k // 512, 16))
    for p in range(k // 512):
        a[p, :8] = np.random.permutation(np.resize(levels, 8))
        for g in range(8):
            far = levels[np.abs(levels - a[p, g]) >= 10]
            a[p, g + 8] = far[np.random.randint(len(far))]
    return np.exp2(a.ravel()).repeat(32)


BF16 = ml_dtypes.bfloat16


def bf(x):
    return np.asarray(x, np.float32).astype(BF16)


def f64(x):
    return np.asarray(x).astype(np.float64)


E2M1 = np.array([0.0, 0.5, 1.0, 1.5, 2.0, 3.0, 4.0, 6.0, -0.0, -0.5, -1.0, -1.5, -2.0, -3.0, -4.0, -6.0])


def pack_weight(w, fmt):
    k, n = w.shape
    w = f64(bf(w)).reshape(k // 32, 32, n)
    amax = np.abs(w).max(1)
    if fmt == "e4m3":
        byte = np.frexp(amax)[1] - 1 + 127 - 7
    else:
        mant, ex = np.frexp(amax / 6.0)
        byte = np.where(mant > 0.5, ex, ex - 1) + 127
    byte = np.clip(np.where(amax > 0, byte, 1), 1, 254)
    scaled = (w * np.exp2(127.0 - byte)[:, None, :]).reshape(k, n).astype(np.float32)
    by_word = np.ascontiguousarray(scaled.reshape(k // 512, 128, 4, n).transpose(0, 1, 3, 2))
    if fmt == "e4m3":
        words = by_word.astype(ml_dtypes.float8_e4m3fn).view(np.uint8)
    else:
        c = by_word.astype(ml_dtypes.float4_e2m1fn).view(np.uint8) & 0xF
        words = c[..., 0::2] | (c[..., 1::2] << 4)
    return np.ascontiguousarray(words), np.ascontiguousarray(byte.astype(np.uint8).reshape(k // 512, 16, n))


def unpack_weight(words, scales, fmt):
    g, p, n, _ = words.shape
    if fmt == "e4m3":
        vals = np.ascontiguousarray(words).view(ml_dtypes.float8_e4m3fn).astype(np.float64)
    else:
        nib = np.empty((g, p, n, 4), np.uint8)
        nib[..., 0::2] = words & 0xF
        nib[..., 1::2] = words >> 4
        vals = E2M1[nib]
    vals = vals * np.repeat(np.exp2(scales.astype(np.float64) - 127.0), 8, axis=1)[..., None]
    return vals.transpose(0, 1, 3, 2).reshape(g * 512, n)
def pack4(w):
    words, scales = pack_weight(w, "e2m1")
    return words.reshape(words.shape[0], 128, -1), scales


def unpack4(words, scales):
    return unpack_weight(words.reshape(words.shape[0], 128, -1, 2), scales, "e2m1")


B, K, F, D = 1024, 2048, 512, 2048


def setup_inputs():
    s, t = mx_kscale(K), mx_kscale(F)
    x_words, x_scales = pack4(np.random.standard_normal((K, B)) * s[:, None])
    phi_words, phi_scales = pack4(np.random.standard_normal((K, F)) / np.sqrt(K) / s[:, None] * t)
    theta_words, theta_scales = pack4(np.random.standard_normal((K, F)) / np.sqrt(K) / s[:, None] * t)
    return {"x_words": x_words, "x_scales": x_scales,
            "phi_words": phi_words, "phi_scales": phi_scales,
            "theta_words": theta_words, "theta_scales": theta_scales,
            "z": bf(np.random.standard_normal(B)),
            "c": bf(0.5 * np.random.standard_normal(F)),
            "gamma": bf(1.0 + 2.0 * np.random.random(F)),
            "load": bf(np.random.standard_normal((F, D)) / np.sqrt(F) / t[:, None]),
            "mu": bf(0.3 * np.random.standard_normal(D))}


def reference(x_words, x_scales, phi_words, phi_scales, theta_words, theta_scales, z, c, gamma, load, mu):
    x = unpack4(x_words, x_scales)
    base = x.T @ unpack4(phi_words, phi_scales)
    shift = x.T @ unpack4(theta_words, theta_scales)
    u = gamma.astype(np.float64) * (f64(z)[:, None] - f64(c))
    gate = 1.0 / (1.0 + np.exp(-u))
    h = base + gate * shift
    y = mxq(h, 1, "e4m3") @ mxq(f64(load), 0, "e4m3")
    return y + f64(mu)

@@ -1,0 +1,309 @@
+from contextlib import ExitStack
+
+import concourse.mybir as mybir
+from concourse.masks import make_identity
+
+F32 = mybir.dt.float32
+BF16 = mybir.dt.bfloat16
+I32 = mybir.dt.int32
+U32 = mybir.dt.uint32
+U8 = mybir.dt.uint8
+FP4X4 = mybir.dt.float4_e2m1fn_x4
+FP8X4 = mybir.dt.float8_e4m3fn_x4
+ACTF = mybir.ActivationFunctionType
+ALU = mybir.AluOpType
+
+B, K, F, D = 1024, 2048, 512, 2048
+P = 128
+G = K // 512
+T = 4
+NQ = 512
+FLOPS = 2 * B * K * F * 2 + 2 * B * F * D
+
+CHUNKS = [(0, 256), (256, 256), (512, 256), (768, 128), (896, 128)]
+
+
+def tile_smooth_transition_autoregression_s4_kernel(
+    tc, x_words, x_scales, phi_words, phi_scales, theta_words, theta_scales, z, c, gamma, load, mu, out
+):
+    nc = tc.nc
+    with ExitStack() as ctx:
+        keep = ctx.enter_context(tc.tile_pool(name="keep", bufs=1))
+        tpool = ctx.enter_context(tc.tile_pool(name="tpool", bufs=6))
+        opool = ctx.enter_context(tc.tile_pool(name="opool", bufs=10))
+        cpool = ctx.enter_context(tc.tile_pool(name="cpool", bufs=6))
+        ps1 = ctx.enter_context(tc.psum_pool(name="ps1", bufs=4))
+        ps2 = ctx.enter_context(tc.psum_pool(name="ps2", bufs=4))
+        ctx.enter_context(tc.manual_schedule())
+
+        th_raw = keep.tile([P, G * F * 2], U8, name="th_raw", align_bytes=64)
+        ph_raw = keep.tile([P, G * F * 2], U8, name="ph_raw", align_bytes=64)
+        th_w = keep.tile([P, G * F * 2], U8, name="th_w", align_bytes=64)
+        ph_w = keep.tile([P, G * F * 2], U8, name="ph_w", align_bytes=64)
+        ths_raw = keep.tile([P, G * F], U8, name="ths_raw", align_bytes=64)
+        phs_raw = keep.tile([P, G * F], U8, name="phs_raw", align_bytes=64)
+        th_s = keep.tile([P, G * F], U8, name="th_s", align_bytes=64)
+        ph_s = keep.tile([P, G * F], U8, name="ph_s", align_bytes=64)
+        xa = keep.tile([P, G * 1024], U8, name="xa", align_bytes=64)
+        xb = keep.tile([P, G * 1024], U8, name="xb", align_bytes=64)
+        xs = keep.tile([P, G * B], U8, name="xs", align_bytes=64)
+        lraw = [keep.tile([P, T, D // 2], BF16, name=f"lraw{h}", align_bytes=64) for h in range(2)]
+        lgrp = [keep.tile([P, NQ, T], BF16, name=f"lgrp{q}", align_bytes=64) for q in range(4)]
+        lq = [keep.tile([P, NQ], U32, name=f"lq{q}", align_bytes=64) for q in range(4)]
+        lqs = [keep.tile([P, NQ], U8, name=f"lqs{q}", align_bytes=64) for q in range(4)]
+        ident = keep.tile([P, P], BF16, name="ident", align_bytes=64)
+        zc = keep.tile([P, 8], BF16, name="zc", align_bytes=64)
+        muc = keep.tile([P, 16], BF16, name="muc", align_bytes=64)
+        gc = keep.tile([P, P], BF16, name="gc", align_bytes=64)
+        gam = keep.tile([P, T], F32, name="gam", align_bytes=64)
+        nb = keep.tile([P, T], F32, name="nb", align_bytes=64)
+        mub = keep.tile([P, D], BF16, name="mub", align_bytes=64)
+        gate = keep.tile([P, T, B], F32, name="gate", align_bytes=64)
+        dum = keep.tile([P, 2], F32, name="dum", align_bytes=64)
+        hg = [keep.tile([P, w, T], BF16, name=f"hg{i}", align_bytes=64) for i, (b0, w) in enumerate(CHUNKS)]
+        hq = [keep.tile([P, w], U32, name=f"hq{i}", align_bytes=64) for i, (b0, w) in enumerate(CHUNKS)]
+        hqs = [keep.tile([P, w], U8, name=f"hqs{i}", align_bytes=64) for i, (b0, w) in enumerate(CHUNKS)]
+
+        def load_words(tile, dram, lo, hi, queue=nc.sync):
+            queue.dma_start(
+                out=tile[:].bitcast(I32).rearrange("p (g n) -> p g n", g=G),
+                in_=dram[:, :, lo:hi].bitcast(I32).rearrange("g p n -> p g n"),
+            )
+
+        def load_scales(tile, dram, rows, queue):
+            view = dram.bitcast(I32).rearrange("g (q r) n -> r q g n", r=4)
+            for r in rows:
+                queue.dma_start(
+                    out=tile[r:P:32, :].bitcast(I32).rearrange("p (g n) -> p g n", g=G),
+                    in_=view[r],
+                )
+
+        load_v = load.rearrange("(a t i) d -> i a t d", t=4, i=4)
+
+        def load_half(h, queue):
+            for i in range(4):
+                queue.dma_start(
+                    out=lraw[h][i:P:4, :, :], in_=load_v[i][:, :, D // 2 * h : D // 2 * (h + 1)]
+                )
+
+        def load_vec(row, dram):
+            nc.scalar.dma_start(
+                out=gc[row : row + 4, :].rearrange("t (a i) -> t a i", i=4),
+                in_=dram.rearrange("(a t i) -> t a i", t=4, i=4),
+            )
+
+        nc.gpsimd.dma_start(out=zc[:], in_=z.rearrange("(p c) -> p c", c=8))
+        nc.vector.memset(gc[:].bitcast(I32), 0)
+        nc.vector.memset(dum[:], 0.0)
+        nc.vector.memset(ths_raw[:].bitcast(I32), 0)
+        nc.vector.memset(xs[:].bitcast(I32), 0)
+        nc.vector.memset(phs_raw[:].bitcast(I32), 0)
+        load_vec(0, gamma)
+        load_vec(4, c)
+        nc.scalar.dma_start(out=muc[:], in_=mu.rearrange("(p c) -> p c", c=16))
+        nc.scalar.activation(out=dum[:, 0:1], in_=dum[:, 1:2], func=ACTF.Sigmoid)
+        load_words(th_raw, theta_words, 0, 1024)
+        load_words(xa, x_words, 0, 1024)
+        load_scales(ths_raw, theta_scales, range(4), nc.sync)
+        load_scales(xs, x_scales, (0, 1), nc.sync)
+        make_identity(nc, ident[:])
+        load_scales(xs, x_scales, (2, 3), nc.gpsimd)
+        load_words(ph_raw, phi_words, 0, 1024, nc.gpsimd)
+        load_scales(phs_raw, phi_scales, range(4), nc.sync)
+        load_half(0, nc.gpsimd)
+        load_half(1, nc.sync)
+        load_words(xb, x_words, 1024, 2048)
+
+        def permute_words(dst, src, g0, g1):
+            nc.vector.tensor_copy(
+                out=dst[:, 1024 * g0 : 1024 * g1].bitcast(I32).rearrange("p (g t a w) -> p g t a w", t=4, a=32, w=2),
+                in_=src[:, 1024 * g0 : 1024 * g1].bitcast(I32).rearrange("p (g a t w) -> p g t a w", t=4, a=32, w=2),
+            )
+
+        def permute_scales(dst, src):
+            nc.vector.tensor_copy(
+                out=dst[:].bitcast(I32).rearrange("p (g t a) -> p g t a", t=4, a=32),
+                in_=src[:].bitcast(I32).rearrange("p (g a t) -> p g t a", t=4, a=32),
+            )
+
+        gcp = ps2.tile([P, P], BF16, name="acc2")
+        nc.tensor.transpose(gcp[:], gc[:], ident[:])
+        zp = ps2.tile([P, 8, P], BF16, name="acc2")
+        for j in range(8):
+            nc.tensor.transpose(zp[:, j, :], zc[:, j : j + 1].to_broadcast([P, P]), ident[:])
+        nc.vector.tensor_copy(out=gam[:], in_=gcp[:, 0:4])
+        nc.vector.scalar_tensor_tensor(out=nb[:], in0=gcp[:, 4:8], scalar=-1.0, in1=gam[:], op0=ALU.mult, op1=ALU.mult)
+
+        def gates(b0, b1):
+            for t in range(T):
+                nc.scalar.activation(
+                    out=gate[:, t, b0:b1].rearrange("p (n c) -> p n c", c=8),
+                    in_=zp[:, :, b0 // 8 : b1 // 8].rearrange("p c n -> p n c"),
+                    func=ACTF.Sigmoid,
+                    bias=nb[:, t : t + 1],
+                    scale=gam[:, t : t + 1],
+                )
+
+        def mu_rows(h):
+            mp = ps2.tile([P, 8, P], BF16, name="acc2")
+            for j in range(8):
+                nc.tensor.transpose(mp[:, j, :], muc[:, 8 * h + j : 8 * h + j + 1].to_broadcast([P, P]), ident[:])
+            return mp
+
+        def mu_copy():
+            for h in range(2):
+                nc.scalar.copy(
+                    out=mub[:].rearrange("p (n k c) -> p k n c", k=2, c=8)[:, h, :, :],
+                    in_=mu_ps[h][:].rearrange("p c n -> p n c"),
+                )
+
+        gates(0, 256)
+        gates(256, 1024)
+        permute_words(th_w, th_raw, 0, 2)
+        permute_words(th_w, th_raw, 2, 4)
+        permute_scales(th_s, ths_raw)
+        mu_ps = [mu_rows(h) for h in range(2)]
+
+        def x_cols(ci, g):
+            b0, w = CHUNKS[ci]
+            tile = xa if b0 < 512 else xb
+            off = 1024 * g + 2 * (b0 % 512)
+            return tile[:, off : off + 2 * w]
+
+        def stage1(ci, kind, ts):
+            b0, w = CHUNKS[ci]
+            words, scales = (th_w, th_s) if kind == "shift" else (ph_w, ph_s)
+            acc = ps1.tile([P, len(ts), w], F32, name="acc1")
+            for j, t in enumerate(ts):
+                for g in range(G):
+                    nc.tensor.matmul_mx(
+                        out=acc[:, j, :],
+                        lhsT=words[:, 1024 * g + 256 * t : 1024 * g + 256 * (t + 1)].bitcast(FP4X4),
+                        lhsT_scale=scales[:, F * g + P * t : F * g + P * (t + 1)],
+                        rhs=x_cols(ci, g).bitcast(FP4X4),
+                        rhs_scale=xs[:, B * g + b0 : B * g + b0 + w],
+                        start=(g == 0),
+                        stop=(g == G - 1),
+                    )
+            return acc
+
+        gated, accs = {}, {}
+
+        def do_shift(ci, ts):
+            b0, w = CHUNKS[ci]
+            acc = accs["s", ci, ts]
+            gs = tpool.tile([P, w, len(ts)], F32, name="gs")
+            nc.vector.tensor_tensor(
+                out=gs[:],
+                in0=acc[:].rearrange("p t b -> p b t"),
+                in1=gate[:, ts[0] : ts[-1] + 1, b0 : b0 + w].rearrange("p t b -> p b t"),
+                op=ALU.mult,
+            )
+            gated[(ci, ts[0])] = gs
+
+        def do_base(ci, ts):
+            acc = accs["b", ci, ts]
+            nc.vector.tensor_tensor(
+                out=hg[ci][:, :, ts[0] : ts[-1] + 1],
+                in0=acc[:].rearrange("p t b -> p b t"),
+                in1=gated[(ci, ts[0])][:],
+                op=ALU.add,
+            )
+
+        def quant_h(ci):
+            nc.vector.quantize_mx(
+                out=hq[ci][:].bitcast(FP8X4), scales=hqs[ci][:], in_=hg[ci][:].rearrange("p b t -> p (b t)")
+            )
+
+        def group_load(q, engine):
+            dst = lgrp[q][:]
+            src = lraw[q // 2][:, :, NQ * (q % 2) : NQ * (q % 2 + 1)].rearrange("p t d -> p d t")
+            if engine == "scalar":
+                nc.scalar.copy(out=dst, in_=src)
+            elif engine == "vector":
+                nc.vector.tensor_copy(out=dst, in_=src)
+            else:
+                nc.gpsimd.tensor_scalar(out=dst, in0=src, scalar1=1.0, scalar2=0.0, op0=ALU.mult, op1=ALU.add)
+
+        def quant_load(q):
+            nc.vector.quantize_mx(
+                out=lq[q][:].bitcast(FP8X4), scales=lqs[q][:], in_=lgrp[q][:].rearrange("p d t -> p (d t)")
+            )
+
+        outs, banks, parts, done = {}, {}, {}, {}
+
+        def stage2(ci, bt, q):
+            acc = ps2.tile([P, NQ], F32, name="acc2")
+            nc.tensor.matmul_mx(
+                out=acc[:],
+                lhsT=hq[ci][:, P * bt : P * (bt + 1)].bitcast(FP8X4),
+                lhsT_scale=hqs[ci][:, P * bt : P * (bt + 1)],
+                rhs=lq[q][:].bitcast(FP8X4),
+                rhs_scale=lqs[q][:],
+                start=True,
+                stop=True,
+            )
+            banks[ci, bt, q] = acc
+
+        def out_cols(ci, bt, q):
+            if (ci, bt, q // 2) not in outs:
+                ob = opool.tile([P, 1024], F32, name="ob")
+                outs[ci, bt, q // 2] = ob
+                done[ci, bt, q // 2] = 0
+            return outs[ci, bt, q // 2][:, NQ * (q % 2) : NQ * (q % 2 + 1)]
+
+        def finished(ci, bt, q):
+            key = (ci, bt, q // 2)
+            done[key] += 1
+            if done[key] == 2:
+                row = CHUNKS[ci][0] + P * bt
+                nc.sync.dma_start(out=out[row : row + P, 1024 * (q // 2) : 1024 * (q // 2 + 1)], in_=outs[key][:])
+
+        def add_mu(ci, bt, q):
+            nc.vector.tensor_tensor(
+                out=out_cols(ci, bt, q), in0=banks[ci, bt, q][:], in1=mub[:, NQ * q : NQ * (q + 1)], op=ALU.add
+            )
+            finished(ci, bt, q)
+
+        def copy_out(ci, bt, q):
+            cp = cpool.tile([P, NQ], F32, name="cp")
+            nc.scalar.copy(out=cp[:], in_=banks[ci, bt, q][:])
+            parts[ci, bt, q] = cp
+
+        def add_mu_copied(ci, bt, q):
+            nc.gpsimd.tensor_tensor(
+                out=out_cols(ci, bt, q), in0=parts[ci, bt, q][:], in1=mub[:, NQ * q : NQ * (q + 1)], op=ALU.add
+            )
+            finished(ci, bt, q)
+
+        STEPS = """
+        s0a s1a vs0a p s0b m vs1a g0g b0b vs0b g1s b0a vb0b s1b vb0a g2s l1 b2a q0 vs1b f001 f011 l0 g3s s2a
+        e011 e001 f000 f010 vs2a b1b c000 l3 c010 a000 b1a l2 vb1b f013 a010 f012 vb1a c013 f002 f003 c012
+        s2b e002 a013 c003 q1 vb2a f111 a003 f103 f110 e111 c103 f100 b2b e110 c100 a012 vs2b f112 f113 a103
+        vb2b f102 c113 f101 s3 e102 c101 a113 q2 e112 f200 f210 a101 vs3 f201 f211 c201 e210 b3 a100 e211
+        e200 f213 f212 a201 e213 f202 c212 f203 e202 s4 c203 a212 vb3 b4 q3 vs4 a203 f301 vb4 f302 f300 e302
+        f303 c300 e303 a300 q4 e301 f403 f400 c403 f401 e400 f402 a403 e401 e402
+        """.split()
+        SLOTS = {"a": (0, 1), "b": (2, 3)}
+        for tok in STEPS:
+            k = tok[0]
+            if k in "sb":
+                ts = SLOTS.get(tok[-1], (0, 1, 2, 3))
+                accs[k, int(tok[1]), ts] = stage1(int(tok[1]), "shift" if k == "s" else "base", ts)
+            elif k == "v":
+                ts = SLOTS.get(tok[-1], (0, 1, 2, 3))
+                (do_shift if tok[1] == "s" else do_base)(int(tok[2]), ts)
+            elif k == "p":
+                permute_words(ph_w, ph_raw, 0, 2)
+                permute_words(ph_w, ph_raw, 2, 4)
+                permute_scales(ph_s, phs_raw)
+            elif k == "m":
+                mu_copy()
+            elif k == "g":
+                group_load(int(tok[1]), {"s": "scalar", "v": "vector", "g": "gpsimd"}[tok[2]])
+            elif k == "l":
+                quant_load(int(tok[1]))
+            elif k == "q":
+                quant_h(int(tok[1]))
+            else:
+                {"f": stage2, "e": add_mu, "c": copy_out, "a": add_mu_copied}[k](*[int(ch) for ch in tok[1:]])

@@ -44,17 +44,14 @@ def tile_smooth_transition_autoregression_s4_kernel(
         phs_raw = keep.tile([P, G * F], U8, name="phs_raw", align_bytes=64)
         th_s = keep.tile([P, G * F], U8, name="th_s", align_bytes=64)
         ph_s = keep.tile([P, G * F], U8, name="ph_s", align_bytes=64)
-        xa = keep.tile([P, G * 1024], U8, name="xa", align_bytes=64)
-        xb = keep.tile([P, G * 1024], U8, name="xb", align_bytes=64)
+        xa = keep.tile([P, G * 512], U8, name="xa", align_bytes=64)
+        xb = keep.tile([P, G * 1536], U8, name="xb", align_bytes=64)
         xs = keep.tile([P, G * B], U8, name="xs", align_bytes=64)
         lraw = [keep.tile([P, T, D // 2], BF16, name=f"lraw{h}", align_bytes=64) for h in range(2)]
         lgrp = [keep.tile([P, NQ, T], BF16, name=f"lgrp{q}", align_bytes=64) for q in range(4)]
         lq = [keep.tile([P, NQ], U32, name=f"lq{q}", align_bytes=64) for q in range(4)]
         lqs = [keep.tile([P, NQ], U8, name=f"lqs{q}", align_bytes=64) for q in range(4)]
         ident = keep.tile([P, P], BF16, name="ident", align_bytes=64)
-        zc = keep.tile([P, 8], BF16, name="zc", align_bytes=64)
-        muc = keep.tile([P, 16], BF16, name="muc", align_bytes=64)
-        gc = keep.tile([P, P], BF16, name="gc", align_bytes=64)
         gam = keep.tile([P, T], F32, name="gam", align_bytes=64)
         nb = keep.tile([P, T], F32, name="nb", align_bytes=64)
         mub = keep.tile([P, D], BF16, name="mub", align_bytes=64)
@@ -86,33 +83,32 @@ def tile_smooth_transition_autoregression_s4_kernel(
                     out=lraw[h][i:P:4, :, :], in_=load_v[i][:, :, D // 2 * h : D // 2 * (h + 1)]
                 )
 
-        def load_vec(row, dram):
-            nc.scalar.dma_start(
-                out=gc[row : row + 4, :].rearrange("t (a i) -> t a i", i=4),
-                in_=dram.rearrange("(a t i) -> t a i", t=4, i=4),
-            )
-
-        nc.gpsimd.dma_start(out=zc[:], in_=z.rearrange("(p c) -> p c", c=8))
-        nc.vector.memset(gc[:].bitcast(I32), 0)
+        vrow = keep.tile([P, P], BF16, name="vrow", align_bytes=64)
+        mrow = keep.tile([P, P], BF16, name="mrow", align_bytes=64)
+        nc.vector.memset(vrow[:].bitcast(I32), 0)
+        nc.vector.memset(mrow[:].bitcast(I32), 0)
         nc.vector.memset(dum[:], 0.0)
         nc.vector.memset(ths_raw[:].bitcast(I32), 0)
         nc.vector.memset(xs[:].bitcast(I32), 0)
         nc.vector.memset(phs_raw[:].bitcast(I32), 0)
-        load_vec(0, gamma)
-        load_vec(4, c)
-        nc.scalar.dma_start(out=muc[:], in_=mu.rearrange("(p c) -> p c", c=16))
+        make_identity(nc, ident[:])
+        for row, vec in ((0, gamma), (4, c)):
+            nc.scalar.dma_start(
+                out=vrow[row : row + 4, :].rearrange("t (a i) -> t a i", i=4),
+                in_=vec.rearrange("(a t i) -> t a i", t=4, i=4),
+            )
+        nc.scalar.dma_start(out=vrow[8:16, :], in_=z.rearrange("(c n) -> c n", n=P))
+        nc.scalar.dma_start(out=mrow[0:16, :], in_=mu.rearrange("(c n) -> c n", n=P))
         nc.scalar.activation(out=dum[:, 0:1], in_=dum[:, 1:2], func=ACTF.Sigmoid)
         load_words(th_raw, theta_words, 0, 1024)
-        load_words(xa, x_words, 0, 1024)
+        load_words(xa, x_words, 0, 512)
         load_scales(ths_raw, theta_scales, range(4), nc.sync)
-        load_scales(xs, x_scales, (0, 1), nc.sync)
-        make_identity(nc, ident[:])
-        load_scales(xs, x_scales, (2, 3), nc.gpsimd)
-        load_words(ph_raw, phi_words, 0, 1024, nc.gpsimd)
-        load_scales(phs_raw, phi_scales, range(4), nc.sync)
+        load_scales(xs, x_scales, range(4), nc.sync)
         load_half(0, nc.gpsimd)
+        load_words(ph_raw, phi_words, 0, 1024)
+        load_scales(phs_raw, phi_scales, range(4), nc.sync)
+        load_words(xb, x_words, 512, 2048)
         load_half(1, nc.sync)
-        load_words(xb, x_words, 1024, 2048)
 
         def permute_words(dst, src, g0, g1):
             nc.vector.tensor_copy(
@@ -122,53 +118,58 @@ def tile_smooth_transition_autoregression_s4_kernel(
 
         def permute_scales(dst, src):
             nc.vector.tensor_copy(
-                out=dst[:].bitcast(I32).rearrange("p (g t a) -> p g t a", t=4, a=32),
-                in_=src[:].bitcast(I32).rearrange("p (g a t) -> p g t a", t=4, a=32),
+                out=dst[:].bitcast(I32).rearrange("p (g t a) -> p g a t", t=4, a=32),
+                in_=src[:].bitcast(I32).rearrange("p (g a t) -> p g a t", t=4, a=32),
             )
 
-        gcp = ps2.tile([P, P], BF16, name="acc2")
-        nc.tensor.transpose(gcp[:], gc[:], ident[:])
-        zp = ps2.tile([P, 8, P], BF16, name="acc2")
-        for j in range(8):
-            nc.tensor.transpose(zp[:, j, :], zc[:, j : j + 1].to_broadcast([P, P]), ident[:])
-        nc.vector.tensor_copy(out=gam[:], in_=gcp[:, 0:4])
-        nc.vector.scalar_tensor_tensor(out=nb[:], in0=gcp[:, 4:8], scalar=-1.0, in1=gam[:], op0=ALU.mult, op1=ALU.mult)
+        def columns(rows, n):
+            cps = ps2.tile([P, P], BF16, name="acc2")
+            nc.tensor.transpose(cps[:], rows[:], ident[:])
+            cols = keep.tile([P, n], BF16, name="cols%d" % n, align_bytes=64)
+            nc.vector.tensor_copy(out=cols[:], in_=cps[:, 0:n])
+            return cols
+
+        def spread(cols, j0):
+            bps = ps2.tile([P, 8, P], BF16, name="acc2")
+            for j in range(8):
+                nc.tensor.transpose(bps[:, j, :], cols[:, j0 + j : j0 + j + 1].to_broadcast([P, P]), ident[:])
+            return bps
+
+        vcols = columns(vrow, 32)
+        nc.vector.tensor_copy(out=gam[:], in_=vcols[:, 0:4])
+        zp = spread(vcols, 8)
+        nc.vector.scalar_tensor_tensor(out=nb[:], in0=vcols[:, 4:8], scalar=-1.0, in1=gam[:], op0=ALU.mult, op1=ALU.mult)
 
         def gates(b0, b1):
             for t in range(T):
                 nc.scalar.activation(
-                    out=gate[:, t, b0:b1].rearrange("p (n c) -> p n c", c=8),
-                    in_=zp[:, :, b0 // 8 : b1 // 8].rearrange("p c n -> p n c"),
+                    out=gate[:, t, b0:b1],
+                    in_=zp[:].rearrange("p c n -> p (c n)")[:, b0:b1],
                     func=ACTF.Sigmoid,
                     bias=nb[:, t : t + 1],
                     scale=gam[:, t : t + 1],
                 )
 
-        def mu_rows(h):
-            mp = ps2.tile([P, 8, P], BF16, name="acc2")
-            for j in range(8):
-                nc.tensor.transpose(mp[:, j, :], muc[:, 8 * h + j : 8 * h + j + 1].to_broadcast([P, P]), ident[:])
-            return mp
-
         def mu_copy():
             for h in range(2):
                 nc.scalar.copy(
-                    out=mub[:].rearrange("p (n k c) -> p k n c", k=2, c=8)[:, h, :, :],
-                    in_=mu_ps[h][:].rearrange("p c n -> p n c"),
+                    out=mub[:, 1024 * h : 1024 * (h + 1)],
+                    in_=mu_ps[h][:].rearrange("p c n -> p (c n)"),
                 )
 
-        gates(0, 256)
-        gates(256, 1024)
+        mcols = columns(mrow, 16)
+        mu_ps = [spread(mcols, 8 * h) for h in range(2)]
         permute_words(th_w, th_raw, 0, 2)
         permute_words(th_w, th_raw, 2, 4)
         permute_scales(th_s, ths_raw)
-        mu_ps = [mu_rows(h) for h in range(2)]
 
         def x_cols(ci, g):
             b0, w = CHUNKS[ci]
-            tile = xa if b0 < 512 else xb
-            off = 1024 * g + 2 * (b0 % 512)
-            return tile[:, off : off + 2 * w]
+            if b0 < 256:
+                off = 512 * g + 2 * b0
+                return xa[:, off : off + 2 * w]
+            off = 1536 * g + 2 * (b0 - 256)
+            return xb[:, off : off + 2 * w]
 
         def stage1(ci, kind, ts):
             b0, w = CHUNKS[ci]
@@ -216,14 +217,12 @@ def tile_smooth_transition_autoregression_s4_kernel(
             )
 
         def group_load(q, engine):
-            dst = lgrp[q][:]
-            src = lraw[q // 2][:, :, NQ * (q % 2) : NQ * (q % 2 + 1)].rearrange("p t d -> p d t")
+            dst = lgrp[q][:].rearrange("p (n i) t -> p n t i", i=4)
+            src = lraw[q // 2][:, :, NQ * (q % 2) : NQ * (q % 2 + 1)].rearrange("p t (n i) -> p n t i", i=4)
             if engine == "scalar":
                 nc.scalar.copy(out=dst, in_=src)
-            elif engine == "vector":
-                nc.vector.tensor_copy(out=dst, in_=src)
             else:
-                nc.gpsimd.tensor_scalar(out=dst, in0=src, scalar1=1.0, scalar2=0.0, op0=ALU.mult, op1=ALU.add)
+                nc.vector.tensor_copy(out=dst, in_=src)
 
         def quant_load(q):
             nc.vector.quantize_mx(
@@ -231,6 +230,7 @@ def tile_smooth_transition_autoregression_s4_kernel(
             )
 
         outs, banks, parts, done = {}, {}, {}, {}
+        LATE = [(4, 0, 1), (4, 0, 0)]
 
         def stage2(ci, bt, q):
             acc = ps2.tile([P, NQ], F32, name="acc2")
@@ -255,8 +255,10 @@ def tile_smooth_transition_autoregression_s4_kernel(
         def finished(ci, bt, q):
             key = (ci, bt, q // 2)
             done[key] += 1
-            if done[key] == 2:
-                row = CHUNKS[ci][0] + P * bt
+            row = CHUNKS[ci][0] + P * bt
+            if key in LATE:
+                nc.sync.dma_start(out=out[row : row + P, NQ * q : NQ * (q + 1)], in_=out_cols(ci, bt, q))
+            elif done[key] == 2:
                 nc.sync.dma_start(out=out[row : row + P, 1024 * (q // 2) : 1024 * (q // 2 + 1)], in_=outs[key][:])
 
         def add_mu(ci, bt, q):
@@ -277,12 +279,12 @@ def tile_smooth_transition_autoregression_s4_kernel(
             finished(ci, bt, q)
 
         STEPS = """
-        s0a s1a vs0a p s0b m vs1a g0g b0b vs0b g1s b0a vb0b s1b vb0a g2s l1 b2a q0 vs1b f001 f011 l0 g3s s2a
-        e011 e001 f000 f010 vs2a b1b c000 l3 c010 a000 b1a l2 vb1b f013 a010 f012 vb1a c013 f002 f003 c012
-        s2b e002 a013 c003 q1 vb2a f111 a003 f103 f110 e111 c103 f100 b2b e110 c100 a012 vs2b f112 f113 a103
-        vb2b f102 c113 f101 s3 e102 c101 a113 q2 e112 f200 f210 a101 vs3 f201 f211 c201 e210 b3 a100 e211
-        e200 f213 f212 a201 e213 f202 c212 f203 e202 s4 c203 a212 vb3 b4 q3 vs4 a203 f301 vb4 f302 f300 e302
-        f303 c300 e303 a300 q4 e301 f403 f400 c403 f401 e400 f402 a403 e401 e402
+        x m s0b y g1v s0a p vs0a b0a vs0b g0s l1 b0b vb0a s1a vb0b g3s l0 s1b vs1a q0 s2b vs1b g2s l3 f001
+        f000 vs2b f011 b1a e000 e001 c011 f003 l2 f013 f010 a011 e003 c013 b1b e010 vb1a a013 s2a vb1b f002
+        b2b vs2a q1 e002 f101 f100 vb2b c101 f112 f113 c112 b2a a101 e100 e113 f102 a112 vb2a f012 f103 s3
+        e012 c103 q2 a103 e102 f210 f202 vs3 f201 c202 f211 e210 b3 a202 e201 e211 f203 vb3 f200 c203 f111
+        e200 f110 s4 a203 e111 e110 f213 q3 f212 vs4 f303 f302 e212 c303 b4 e213 a303 e302 f300 vb4 f301 e300
+        q4 e301 f401 f403 e401 f400 c403 f402 e400 a403 e402
         """.split()
         SLOTS = {"a": (0, 1), "b": (2, 3)}
         for tok in STEPS:
@@ -297,6 +299,10 @@ def tile_smooth_transition_autoregression_s4_kernel(
                 permute_words(ph_w, ph_raw, 0, 2)
                 permute_words(ph_w, ph_raw, 2, 4)
                 permute_scales(ph_s, phs_raw)
+            elif k == "x":
+                gates(0, 256)
+            elif k == "y":
+                gates(256, 1024)
             elif k == "m":
                 mu_copy()
             elif k == "g":

@@ -32,8 +32,7 @@ def tile_smooth_transition_autoregression_s4_kernel(
         tpool = ctx.enter_context(tc.tile_pool(name="tpool", bufs=6))
         opool = ctx.enter_context(tc.tile_pool(name="opool", bufs=10))
         cpool = ctx.enter_context(tc.tile_pool(name="cpool", bufs=6))
-        ps1 = ctx.enter_context(tc.psum_pool(name="ps1", bufs=4))
-        ps2 = ctx.enter_context(tc.psum_pool(name="ps2", bufs=4))
+        psum = ctx.enter_context(tc.psum_pool(name="psum", bufs=1))
         ctx.enter_context(tc.manual_schedule())
 
         th_raw = keep.tile([P, G * F * 2], U8, name="th_raw", align_bytes=64)
@@ -45,8 +44,10 @@ def tile_smooth_transition_autoregression_s4_kernel(
         th_s = keep.tile([P, G * F], U8, name="th_s", align_bytes=64)
         ph_s = keep.tile([P, G * F], U8, name="ph_s", align_bytes=64)
         xa = keep.tile([P, G * 512], U8, name="xa", align_bytes=64)
-        xb = keep.tile([P, G * 1536], U8, name="xb", align_bytes=64)
-        xs = keep.tile([P, G * B], U8, name="xs", align_bytes=64)
+        xb = keep.tile([P, G * 512], U8, name="xb", align_bytes=64)
+        xc = keep.tile([P, G * 1024], U8, name="xc", align_bytes=64)
+        xsa = keep.tile([P, G * 256], U8, name="xsa", align_bytes=64)
+        xsb = keep.tile([P, G * 768], U8, name="xsb", align_bytes=64)
         lraw = [keep.tile([P, T, D // 2], BF16, name=f"lraw{h}", align_bytes=64) for h in range(2)]
         lgrp = [keep.tile([P, NQ, T], BF16, name=f"lgrp{q}", align_bytes=64) for q in range(4)]
         lq = [keep.tile([P, NQ], U32, name=f"lq{q}", align_bytes=64) for q in range(4)]
@@ -55,9 +56,11 @@ def tile_smooth_transition_autoregression_s4_kernel(
         gam = keep.tile([P, T], F32, name="gam", align_bytes=64)
         nb = keep.tile([P, T], F32, name="nb", align_bytes=64)
         mub = keep.tile([P, D], BF16, name="mub", align_bytes=64)
-        gate = keep.tile([P, T, B], F32, name="gate", align_bytes=64)
+        gate_a = keep.tile([P, T, 256], F32, name="gate_a", align_bytes=64)
+        gate_b = keep.tile([P, T, 768], F32, name="gate_b", align_bytes=64)
         dum = keep.tile([P, 2], F32, name="dum", align_bytes=64)
         hg = [keep.tile([P, w, T], BF16, name=f"hg{i}", align_bytes=64) for i, (b0, w) in enumerate(CHUNKS)]
+        ht = {i: keep.tile([P, T, CHUNKS[i][1]], BF16, name=f"ht{i}", align_bytes=64) for i in (1, 2)}
         hq = [keep.tile([P, w], U32, name=f"hq{i}", align_bytes=64) for i, (b0, w) in enumerate(CHUNKS)]
         hqs = [keep.tile([P, w], U8, name=f"hqs{i}", align_bytes=64) for i, (b0, w) in enumerate(CHUNKS)]
 
@@ -67,10 +70,10 @@ def tile_smooth_transition_autoregression_s4_kernel(
                 in_=dram[:, :, lo:hi].bitcast(I32).rearrange("g p n -> p g n"),
             )
 
-        def load_scales(tile, dram, rows, queue):
-            view = dram.bitcast(I32).rearrange("g (q r) n -> r q g n", r=4)
-            for r in rows:
-                queue.dma_start(
+        def load_scales(tile, dram, lo, hi):
+            view = dram[:, :, lo:hi].bitcast(I32).rearrange("g (q r) n -> r q g n", r=4)
+            for r in range(4):
+                nc.sync.dma_start(
                     out=tile[r:P:32, :].bitcast(I32).rearrange("p (g n) -> p g n", g=G),
                     in_=view[r],
                 )
@@ -89,8 +92,9 @@ def tile_smooth_transition_autoregression_s4_kernel(
         nc.vector.memset(mrow[:].bitcast(I32), 0)
         nc.vector.memset(dum[:], 0.0)
         nc.vector.memset(ths_raw[:].bitcast(I32), 0)
-        nc.vector.memset(xs[:].bitcast(I32), 0)
+        nc.vector.memset(xsa[:].bitcast(I32), 0)
         nc.vector.memset(phs_raw[:].bitcast(I32), 0)
+        nc.vector.memset(xsb[:].bitcast(I32), 0)
         make_identity(nc, ident[:])
         for row, vec in ((0, gamma), (4, c)):
             nc.scalar.dma_start(
@@ -101,14 +105,16 @@ def tile_smooth_transition_autoregression_s4_kernel(
         nc.scalar.dma_start(out=mrow[0:16, :], in_=mu.rearrange("(c n) -> c n", n=P))
         nc.scalar.activation(out=dum[:, 0:1], in_=dum[:, 1:2], func=ACTF.Sigmoid)
         load_words(th_raw, theta_words, 0, 1024)
+        load_scales(ths_raw, theta_scales, 0, F)
+        load_scales(xsa, x_scales, 0, 256)
         load_words(xa, x_words, 0, 512)
-        load_scales(ths_raw, theta_scales, range(4), nc.sync)
-        load_scales(xs, x_scales, range(4), nc.sync)
-        load_half(0, nc.gpsimd)
         load_words(ph_raw, phi_words, 0, 1024)
-        load_scales(phs_raw, phi_scales, range(4), nc.sync)
-        load_words(xb, x_words, 512, 2048)
+        load_scales(phs_raw, phi_scales, 0, F)
+        load_scales(xsb, x_scales, 256, B)
+        load_words(xb, x_words, 512, 1024)
+        load_half(0, nc.sync)
         load_half(1, nc.sync)
+        load_words(xc, x_words, 1024, 2048)
 
         def permute_words(dst, src, g0, g1):
             nc.vector.tensor_copy(
@@ -122,28 +128,32 @@ def tile_smooth_transition_autoregression_s4_kernel(
                 in_=src[:].bitcast(I32).rearrange("p (g a t) -> p g a t", t=4, a=32),
             )
 
+        def bank_tile(shape, dtype, bank):
+            tile = psum.tile(shape, dtype, name="bank%d" % bank)
+            return tile
+
         def columns(rows, n):
-            cps = ps2.tile([P, P], BF16, name="acc2")
+            cps = bank_tile([P, P], BF16, 0)
             nc.tensor.transpose(cps[:], rows[:], ident[:])
             cols = keep.tile([P, n], BF16, name="cols%d" % n, align_bytes=64)
             nc.vector.tensor_copy(out=cols[:], in_=cps[:, 0:n])
             return cols
 
-        def spread(cols, j0):
-            bps = ps2.tile([P, 8, P], BF16, name="acc2")
+        def spread(cols, j0, bank):
+            bps = bank_tile([P, 8, P], BF16, bank)
             for j in range(8):
                 nc.tensor.transpose(bps[:, j, :], cols[:, j0 + j : j0 + j + 1].to_broadcast([P, P]), ident[:])
             return bps
 
         vcols = columns(vrow, 32)
         nc.vector.tensor_copy(out=gam[:], in_=vcols[:, 0:4])
-        zp = spread(vcols, 8)
+        zp = spread(vcols, 8, 1)
         nc.vector.scalar_tensor_tensor(out=nb[:], in0=vcols[:, 4:8], scalar=-1.0, in1=gam[:], op0=ALU.mult, op1=ALU.mult)
 
-        def gates(b0, b1):
+        def gates(tile, b0, b1):
             for t in range(T):
                 nc.scalar.activation(
-                    out=gate[:, t, b0:b1],
+                    out=tile[:, t, :],
                     in_=zp[:].rearrange("p c n -> p (c n)")[:, b0:b1],
                     func=ACTF.Sigmoid,
                     bias=nb[:, t : t + 1],
@@ -158,23 +168,27 @@ def tile_smooth_transition_autoregression_s4_kernel(
                 )
 
         mcols = columns(mrow, 16)
-        mu_ps = [spread(mcols, 8 * h) for h in range(2)]
+        mu_ps = [spread(mcols, 8 * h, 2 + h) for h in range(2)]
         permute_words(th_w, th_raw, 0, 2)
         permute_words(th_w, th_raw, 2, 4)
         permute_scales(th_s, ths_raw)
 
         def x_cols(ci, g):
             b0, w = CHUNKS[ci]
-            if b0 < 256:
-                off = 512 * g + 2 * b0
-                return xa[:, off : off + 2 * w]
-            off = 1536 * g + 2 * (b0 - 256)
-            return xb[:, off : off + 2 * w]
+            tile, first, width = (xa, 0, 256) if b0 < 256 else (xb, 256, 256) if b0 < 512 else (xc, 512, 512)
+            off = 2 * (width * g + b0 - first)
+            return tile[:, off : off + 2 * w]
 
-        def stage1(ci, kind, ts):
+        def x_scale_cols(ci, g):
+            b0, w = CHUNKS[ci]
+            tile, first, width = (xsa, 0, 256) if b0 < 256 else (xsb, 256, 768)
+            off = width * g + b0 - first
+            return tile[:, off : off + w]
+
+        def stage1(ci, kind, ts, bank):
             b0, w = CHUNKS[ci]
             words, scales = (th_w, th_s) if kind == "shift" else (ph_w, ph_s)
-            acc = ps1.tile([P, len(ts), w], F32, name="acc1")
+            acc = bank_tile([P, len(ts), w], F32, bank)
             for j, t in enumerate(ts):
                 for g in range(G):
                     nc.tensor.matmul_mx(
@@ -182,7 +196,7 @@ def tile_smooth_transition_autoregression_s4_kernel(
                         lhsT=words[:, 1024 * g + 256 * t : 1024 * g + 256 * (t + 1)].bitcast(FP4X4),
                         lhsT_scale=scales[:, F * g + P * t : F * g + P * (t + 1)],
                         rhs=x_cols(ci, g).bitcast(FP4X4),
-                        rhs_scale=xs[:, B * g + b0 : B * g + b0 + w],
+                        rhs_scale=x_scale_cols(ci, g),
                         start=(g == 0),
                         stop=(g == G - 1),
                     )
@@ -193,23 +207,31 @@ def tile_smooth_transition_autoregression_s4_kernel(
         def do_shift(ci, ts):
             b0, w = CHUNKS[ci]
             acc = accs["s", ci, ts]
-            gs = tpool.tile([P, w, len(ts)], F32, name="gs")
-            nc.vector.tensor_tensor(
-                out=gs[:],
-                in0=acc[:].rearrange("p t b -> p b t"),
-                in1=gate[:, ts[0] : ts[-1] + 1, b0 : b0 + w].rearrange("p t b -> p b t"),
-                op=ALU.mult,
-            )
+            tile, first = (gate_a, 0) if b0 < 256 else (gate_b, 256)
+            gates_in = tile[:, ts[0] : ts[-1] + 1, b0 - first : b0 - first + w]
+            if ci in ht:
+                gs = tpool.tile([P, len(ts), w], F32, name="gs")
+                nc.vector.tensor_tensor(out=gs[:], in0=acc[:], in1=gates_in, op=ALU.mult)
+            else:
+                gs = tpool.tile([P, w, len(ts)], F32, name="gs")
+                nc.vector.tensor_tensor(
+                    out=gs[:], in0=acc[:].rearrange("p t b -> p b t"), in1=gates_in.rearrange("p t b -> p b t"), op=ALU.mult
+                )
             gated[(ci, ts[0])] = gs
 
         def do_base(ci, ts):
             acc = accs["b", ci, ts]
-            nc.vector.tensor_tensor(
-                out=hg[ci][:, :, ts[0] : ts[-1] + 1],
-                in0=acc[:].rearrange("p t b -> p b t"),
-                in1=gated[(ci, ts[0])][:],
-                op=ALU.add,
-            )
+            if ci in ht:
+                nc.vector.tensor_tensor(
+                    out=ht[ci][:, ts[0] : ts[-1] + 1, :], in0=acc[:], in1=gated[(ci, ts[0])][:], op=ALU.add
+                )
+            else:
+                nc.vector.tensor_tensor(
+                    out=hg[ci][:, :, ts[0] : ts[-1] + 1],
+                    in0=acc[:].rearrange("p t b -> p b t"),
+                    in1=gated[(ci, ts[0])][:],
+                    op=ALU.add,
+                )
 
         def quant_h(ci):
             nc.vector.quantize_mx(
@@ -230,10 +252,10 @@ def tile_smooth_transition_autoregression_s4_kernel(
             )
 
         outs, banks, parts, done = {}, {}, {}, {}
-        LATE = [(4, 0, 1), (4, 0, 0)]
+        LATE = [(3, 0, 1), (3, 0, 0)]
 
-        def stage2(ci, bt, q):
-            acc = ps2.tile([P, NQ], F32, name="acc2")
+        def stage2(ci, bt, q, bank):
+            acc = bank_tile([P, NQ], F32, bank)
             nc.tensor.matmul_mx(
                 out=acc[:],
                 lhsT=hq[ci][:, P * bt : P * (bt + 1)].bitcast(FP8X4),
@@ -279,19 +301,29 @@ def tile_smooth_transition_autoregression_s4_kernel(
             finished(ci, bt, q)
 
         STEPS = """
-        x m s0b y g1v s0a p vs0a b0a vs0b g0s l1 b0b vb0a s1a vb0b g3s l0 s1b vs1a q0 s2b vs1b g2s l3 f001
-        f000 vs2b f011 b1a e000 e001 c011 f003 l2 f013 f010 a011 e003 c013 b1b e010 vb1a a013 s2a vb1b f002
-        b2b vs2a q1 e002 f101 f100 vb2b c101 f112 f113 c112 b2a a101 e100 e113 f102 a112 vb2a f012 f103 s3
-        e012 c103 q2 a103 e102 f210 f202 vs3 f201 c202 f211 e210 b3 a202 e201 e211 f203 vb3 f200 c203 f111
-        e200 f110 s4 a203 e111 e110 f213 q3 f212 vs4 f303 f302 e212 c303 b4 e213 a303 e302 f300 vb4 f301 e300
-        q4 e301 f401 f403 e401 f400 c403 f402 e400 a403 e402
+        x m s0a.0 s0b.4 y p vs0b b0a.5 vs0a b0b.6 vb0a s1a.7 vb0b g0s g1v b1a.2 q0 s1b.3 l1 vs1a g3s f001.4
+        vs1b f011.0 b1b.1 e001 l0 b2a.5 vb1b c011 l3 g2s f000.6 f010.7 a011 vb1a f013.3 s2b.4 e000 e013
+        f003.1 e010 h1 s2a.0 l2 vs2b c003 f012.2 f002.6 q1 c012 b2b.3 a003 vs2a e002 f103.7 vb2a a012 f110.4
+        c103 f100.1 vb2b f101.2 f113.0 e100 h2 a103 f102.6 f111.5 e101 f112.7 s4.3 e102 c112 q2 c111 e113
+        a112 f211.1 e110 f210.2 c211 f212.6 e210 f213.7 a111 f202.5 e213 b4.0 c202 e212 a211 vs4 f200.4
+        f203.1 vb4 c200 a202 f201.2 s3.7 e203 q4 a200 e201 f401.5 f403.6 vs3 c401 f402.3 f400.0 e403 b3.4
+        a401 e402 e400 vb3 q3 f300.1 f301.2 e300 f303.7 f302.5 e301 e302 e303
         """.split()
         SLOTS = {"a": (0, 1), "b": (2, 3)}
         for tok in STEPS:
             k = tok[0]
             if k in "sb":
-                ts = SLOTS.get(tok[-1], (0, 1, 2, 3))
-                accs[k, int(tok[1]), ts] = stage1(int(tok[1]), "shift" if k == "s" else "base", ts)
+                unit, bank = tok.split(".")
+                ts = SLOTS.get(unit[-1], (0, 1, 2, 3))
+                accs[k, int(unit[1]), ts] = stage1(int(unit[1]), "shift" if k == "s" else "base", ts, int(bank))
+            elif k == "f":
+                stage2(*[int(ch) for ch in tok[1:4]], bank=int(tok[5]))
+            elif k == "h":
+                ci = int(tok[1])
+                nc.scalar.copy(
+                    out=hg[ci][:].rearrange("p (n i) t -> p n t i", i=4),
+                    in_=ht[ci][:].rearrange("p t (n i) -> p n t i", i=4),
+                )
             elif k == "v":
                 ts = SLOTS.get(tok[-1], (0, 1, 2, 3))
                 (do_shift if tok[1] == "s" else do_base)(int(tok[2]), ts)
@@ -300,9 +332,9 @@ def tile_smooth_transition_autoregression_s4_kernel(
                 permute_words(ph_w, ph_raw, 2, 4)
                 permute_scales(ph_s, phs_raw)
             elif k == "x":
-                gates(0, 256)
+                gates(gate_a, 0, 256)
             elif k == "y":
-                gates(256, 1024)
+                gates(gate_b, 256, 1024)
             elif k == "m":
                 mu_copy()
             elif k == "g":
@@ -312,4 +344,4 @@ def tile_smooth_transition_autoregression_s4_kernel(
             elif k == "q":
                 quant_h(int(tok[1]))
             else:
-                {"f": stage2, "e": add_mu, "c": copy_out, "a": add_mu_copied}[k](*[int(ch) for ch in tok[1:]])
+                {"e": add_mu, "c": copy_out, "a": add_mu_copied}[k](*[int(ch) for ch in tok[1:]])

@@ -29,9 +29,9 @@ def tile_smooth_transition_autoregression_s4_kernel(
     nc = tc.nc
     with ExitStack() as ctx:
         keep = ctx.enter_context(tc.tile_pool(name="keep", bufs=1))
-        tpool = ctx.enter_context(tc.tile_pool(name="tpool", bufs=6))
-        opool = ctx.enter_context(tc.tile_pool(name="opool", bufs=10))
-        cpool = ctx.enter_context(tc.tile_pool(name="cpool", bufs=6))
+        tpool = ctx.enter_context(tc.tile_pool(name="tpool", bufs=8))
+        opool = ctx.enter_context(tc.tile_pool(name="opool", bufs=16))
+        cpool = ctx.enter_context(tc.tile_pool(name="cpool", bufs=8))
         psum = ctx.enter_context(tc.psum_pool(name="psum", bufs=1))
         ctx.enter_context(tc.manual_schedule())
 
@@ -70,10 +70,10 @@ def tile_smooth_transition_autoregression_s4_kernel(
                 in_=dram[:, :, lo:hi].bitcast(I32).rearrange("g p n -> p g n"),
             )
 
-        def load_scales(tile, dram, lo, hi):
+        def load_scales(tile, dram, lo, hi, queues):
             view = dram[:, :, lo:hi].bitcast(I32).rearrange("g (q r) n -> r q g n", r=4)
-            for r in range(4):
-                nc.sync.dma_start(
+            for r, queue in enumerate(queues):
+                queue.dma_start(
                     out=tile[r:P:32, :].bitcast(I32).rearrange("p (g n) -> p g n", g=G),
                     in_=view[r],
                 )
@@ -88,14 +88,14 @@ def tile_smooth_transition_autoregression_s4_kernel(
 
         vrow = keep.tile([P, P], BF16, name="vrow", align_bytes=64)
         mrow = keep.tile([P, P], BF16, name="mrow", align_bytes=64)
-        nc.vector.memset(vrow[:].bitcast(I32), 0)
         nc.vector.memset(mrow[:].bitcast(I32), 0)
-        nc.vector.memset(dum[:], 0.0)
+        nc.vector.memset(vrow[:].bitcast(I32), 0)
         nc.vector.memset(ths_raw[:].bitcast(I32), 0)
+        make_identity(nc, ident[:])
         nc.vector.memset(xsa[:].bitcast(I32), 0)
+        nc.vector.memset(dum[:], 0.0)
         nc.vector.memset(phs_raw[:].bitcast(I32), 0)
         nc.vector.memset(xsb[:].bitcast(I32), 0)
-        make_identity(nc, ident[:])
         for row, vec in ((0, gamma), (4, c)):
             nc.scalar.dma_start(
                 out=vrow[row : row + 4, :].rearrange("t (a i) -> t a i", i=4),
@@ -105,16 +105,16 @@ def tile_smooth_transition_autoregression_s4_kernel(
         nc.scalar.dma_start(out=mrow[0:16, :], in_=mu.rearrange("(c n) -> c n", n=P))
         nc.scalar.activation(out=dum[:, 0:1], in_=dum[:, 1:2], func=ACTF.Sigmoid)
         load_words(th_raw, theta_words, 0, 1024)
-        load_scales(ths_raw, theta_scales, 0, F)
-        load_scales(xsa, x_scales, 0, 256)
-        load_words(xa, x_words, 0, 512)
+        load_scales(ths_raw, theta_scales, 0, F, [nc.sync] * 4)
+        load_words(xa, x_words, 0, 512, nc.gpsimd)
+        load_scales(xsa, x_scales, 0, 256, [nc.sync] * 3 + [nc.gpsimd])
         load_words(ph_raw, phi_words, 0, 1024)
-        load_scales(phs_raw, phi_scales, 0, F)
-        load_scales(xsb, x_scales, 256, B)
+        load_scales(phs_raw, phi_scales, 0, F, [nc.sync] * 4)
+        load_scales(xsb, x_scales, 256, B, [nc.gpsimd] * 4)
         load_words(xb, x_words, 512, 1024)
         load_half(0, nc.sync)
-        load_half(1, nc.sync)
         load_words(xc, x_words, 1024, 2048)
+        load_half(1, nc.sync)
 
         def permute_words(dst, src, g0, g1):
             nc.vector.tensor_copy(
@@ -132,8 +132,8 @@ def tile_smooth_transition_autoregression_s4_kernel(
             tile = psum.tile(shape, dtype, name="bank%d" % bank)
             return tile
 
-        def columns(rows, n):
-            cps = bank_tile([P, P], BF16, 0)
+        def columns(rows, n, bank):
+            cps = bank_tile([P, P], BF16, bank)
             nc.tensor.transpose(cps[:], rows[:], ident[:])
             cols = keep.tile([P, n], BF16, name="cols%d" % n, align_bytes=64)
             nc.vector.tensor_copy(out=cols[:], in_=cps[:, 0:n])
@@ -145,9 +145,11 @@ def tile_smooth_transition_autoregression_s4_kernel(
                 nc.tensor.transpose(bps[:, j, :], cols[:, j0 + j : j0 + j + 1].to_broadcast([P, P]), ident[:])
             return bps
 
-        vcols = columns(vrow, 32)
+        vcols = columns(vrow, 32, 0)
+        mcols = columns(mrow, 16, 4)
         nc.vector.tensor_copy(out=gam[:], in_=vcols[:, 0:4])
         zp = spread(vcols, 8, 1)
+        mu_ps = [spread(mcols, 0, 2)]
         nc.vector.scalar_tensor_tensor(out=nb[:], in0=vcols[:, 4:8], scalar=-1.0, in1=gam[:], op0=ALU.mult, op1=ALU.mult)
 
         def gates(tile, b0, b1):
@@ -167,8 +169,6 @@ def tile_smooth_transition_autoregression_s4_kernel(
                     in_=mu_ps[h][:].rearrange("p c n -> p (c n)"),
                 )
 
-        mcols = columns(mrow, 16)
-        mu_ps = [spread(mcols, 8 * h, 2 + h) for h in range(2)]
         permute_words(th_w, th_raw, 0, 2)
         permute_words(th_w, th_raw, 2, 4)
         permute_scales(th_s, ths_raw)
@@ -241,7 +241,17 @@ def tile_smooth_transition_autoregression_s4_kernel(
         def group_load(q, engine):
             dst = lgrp[q][:].rearrange("p (n i) t -> p n t i", i=4)
             src = lraw[q // 2][:, :, NQ * (q % 2) : NQ * (q % 2 + 1)].rearrange("p t (n i) -> p n t i", i=4)
-            if engine == "scalar":
+            if engine == "gpsimd":
+                for n0 in (0, NQ // 8):
+                    nc.gpsimd.tensor_scalar(
+                        out=dst[:, n0 : n0 + NQ // 8],
+                        in0=src[:, n0 : n0 + NQ // 8],
+                        scalar1=1.0,
+                        scalar2=0.0,
+                        op0=ALU.mult,
+                        op1=ALU.add,
+                    )
+            elif engine == "scalar":
                 nc.scalar.copy(out=dst, in_=src)
             else:
                 nc.vector.tensor_copy(out=dst, in_=src)
@@ -301,13 +311,13 @@ def tile_smooth_transition_autoregression_s4_kernel(
             finished(ci, bt, q)
 
         STEPS = """
-        x m s0a.0 s0b.4 y p vs0b b0a.5 vs0a b0b.6 vb0a s1a.7 vb0b g0s g1v b1a.2 q0 s1b.3 l1 vs1a g3s f001.4
-        vs1b f011.0 b1b.1 e001 l0 b2a.5 vb1b c011 l3 g2s f000.6 f010.7 a011 vb1a f013.3 s2b.4 e000 e013
-        f003.1 e010 h1 s2a.0 l2 vs2b c003 f012.2 f002.6 q1 c012 b2b.3 a003 vs2a e002 f103.7 vb2a a012 f110.4
-        c103 f100.1 vb2b f101.2 f113.0 e100 h2 a103 f102.6 f111.5 e101 f112.7 s4.3 e102 c112 q2 c111 e113
-        a112 f211.1 e110 f210.2 c211 f212.6 e210 f213.7 a111 f202.5 e213 b4.0 c202 e212 a211 vs4 f200.4
-        f203.1 vb4 c200 a202 f201.2 s3.7 e203 q4 a200 e201 f401.5 f403.6 vs3 c401 f402.3 f400.0 e403 b3.4
-        a401 e402 e400 vb3 q3 f300.1 f301.2 e300 f303.7 f302.5 e301 e302 e303
+        x y s0b.0 p s0a.4 u vs0b b0b.5 vs0a m b0a.6 vb0b s1a.7 vb0a g1s b1a.0 g0v s4.1 q0 l0 l1 f000.4 f010.5
+        vs4 c000 f001.2 b4.3 vs1a c010 a000 e001 g2s vb1a s2b.6 a010 vb4 f011.1 vs2b s2a.4 q4 c011 l2 f400.7
+        g3s vs2a a011 f401.5 f402.2 s1b.0 e400 e401 b1b.3 vs1b c402 l3 f012.6 f002.1 a402 vb1b c012 f403.4
+        f003.7 e002 f013.5 h1 b2a.0 a012 e003 e403 c013 b2b.2 q1 a013 vb2a f112.3 vb2b f111.6 c112 f110.1
+        f101.7 e111 f113.4 h2 a112 f102.5 e110 f103.0 f100.2 e113 s3.3 c102 q2 e103 a102 f203.6 e100 f213.1
+        c203 f202.4 e101 f200.5 f201.0 a203 c200 f212.2 e202 f211.6 b3.7 c212 e201 a200 vs3 f210.5 e213 a212
+        vb3 e210 q3 e211 f300.4 f303.2 e300 f301.0 c303 f302.3 e301 a303 e302
         """.split()
         SLOTS = {"a": (0, 1), "b": (2, 3)}
         for tok in STEPS:
@@ -335,6 +345,8 @@ def tile_smooth_transition_autoregression_s4_kernel(
                 gates(gate_a, 0, 256)
             elif k == "y":
                 gates(gate_b, 256, 1024)
+            elif k == "u":
+                mu_ps.append(spread(mcols, 8, 3))
             elif k == "m":
                 mu_copy()
             elif k == "g":

from contextlib import ExitStack

import concourse.mybir as mybir
from concourse.masks import make_identity

F32 = mybir.dt.float32
BF16 = mybir.dt.bfloat16
I32 = mybir.dt.int32
U32 = mybir.dt.uint32
U8 = mybir.dt.uint8
FP4X4 = mybir.dt.float4_e2m1fn_x4
FP8X4 = mybir.dt.float8_e4m3fn_x4
ACTF = mybir.ActivationFunctionType
ALU = mybir.AluOpType

B, K, F, D = 1024, 2048, 512, 2048
P = 128
G = K // 512
T = 4
NQ = 512
FLOPS = 2 * B * K * F * 2 + 2 * B * F * D

CHUNKS = [(0, 256), (256, 256), (512, 256), (768, 128), (896, 128)]


def tile_smooth_transition_autoregression_s4_kernel(
    tc, x_words, x_scales, phi_words, phi_scales, theta_words, theta_scales, z, c, gamma, load, mu, out
):
    nc = tc.nc
    with ExitStack() as ctx:
        keep = ctx.enter_context(tc.tile_pool(name="keep", bufs=1))
        tpool = ctx.enter_context(tc.tile_pool(name="tpool", bufs=8))
        opool = ctx.enter_context(tc.tile_pool(name="opool", bufs=16))
        cpool = ctx.enter_context(tc.tile_pool(name="cpool", bufs=8))
        psum = ctx.enter_context(tc.psum_pool(name="psum", bufs=1))
        ctx.enter_context(tc.manual_schedule())

        th_raw = keep.tile([P, G * F * 2], U8, name="th_raw", align_bytes=64)
        ph_raw = keep.tile([P, G * F * 2], U8, name="ph_raw", align_bytes=64)
        th_w = keep.tile([P, G * F * 2], U8, name="th_w", align_bytes=64)
        ph_w = keep.tile([P, G * F * 2], U8, name="ph_w", align_bytes=64)
        ths_raw = keep.tile([P, G * F], U8, name="ths_raw", align_bytes=64)
        phs_raw = keep.tile([P, G * F], U8, name="phs_raw", align_bytes=64)
        th_s = keep.tile([P, G * F], U8, name="th_s", align_bytes=64)
        ph_s = keep.tile([P, G * F], U8, name="ph_s", align_bytes=64)
        xa = keep.tile([P, G * 512], U8, name="xa", align_bytes=64)
        xb = keep.tile([P, G * 512], U8, name="xb", align_bytes=64)
        xc = keep.tile([P, G * 1024], U8, name="xc", align_bytes=64)
        xsa = keep.tile([P, G * 256], U8, name="xsa", align_bytes=64)
        xsb = keep.tile([P, G * 768], U8, name="xsb", align_bytes=64)
        lraw = [keep.tile([P, T, D // 2], BF16, name=f"lraw{h}", align_bytes=64) for h in range(2)]
        lgrp = [keep.tile([P, NQ, T], BF16, name=f"lgrp{q}", align_bytes=64) for q in range(4)]
        lq = [keep.tile([P, NQ], U32, name=f"lq{q}", align_bytes=64) for q in range(4)]
        lqs = [keep.tile([P, NQ], U8, name=f"lqs{q}", align_bytes=64) for q in range(4)]
        ident = keep.tile([P, P], BF16, name="ident", align_bytes=64)
        gam = keep.tile([P, T], F32, name="gam", align_bytes=64)
        nb = keep.tile([P, T], F32, name="nb", align_bytes=64)
        mub = keep.tile([P, D], BF16, name="mub", align_bytes=64)
        gate_a = keep.tile([P, T, 256], F32, name="gate_a", align_bytes=64)
        gate_b = keep.tile([P, T, 768], F32, name="gate_b", align_bytes=64)
        dum = keep.tile([P, 2], F32, name="dum", align_bytes=64)
        hg = [keep.tile([P, w, T], BF16, name=f"hg{i}", align_bytes=64) for i, (b0, w) in enumerate(CHUNKS)]
        ht = {i: keep.tile([P, T, CHUNKS[i][1]], BF16, name=f"ht{i}", align_bytes=64) for i in (1, 2)}
        hq = [keep.tile([P, w], U32, name=f"hq{i}", align_bytes=64) for i, (b0, w) in enumerate(CHUNKS)]
        hqs = [keep.tile([P, w], U8, name=f"hqs{i}", align_bytes=64) for i, (b0, w) in enumerate(CHUNKS)]

        def load_words(tile, dram, lo, hi, queue=nc.sync):
            queue.dma_start(
                out=tile[:].bitcast(I32).rearrange("p (g n) -> p g n", g=G),
                in_=dram[:, :, lo:hi].bitcast(I32).rearrange("g p n -> p g n"),
            )

        def load_scales(tile, dram, lo, hi, queues):
            view = dram[:, :, lo:hi].bitcast(I32).rearrange("g (q r) n -> r q g n", r=4)
            for r, queue in enumerate(queues):
                queue.dma_start(
                    out=tile[r:P:32, :].bitcast(I32).rearrange("p (g n) -> p g n", g=G),
                    in_=view[r],
                )

        load_v = load.rearrange("(a t i) d -> i a t d", t=4, i=4)

        def load_half(h, queue):
            for i in range(4):
                queue.dma_start(
                    out=lraw[h][i:P:4, :, :], in_=load_v[i][:, :, D // 2 * h : D // 2 * (h + 1)]
                )

        vrow = keep.tile([P, P], BF16, name="vrow", align_bytes=64)
        mrow = keep.tile([P, P], BF16, name="mrow", align_bytes=64)
        nc.vector.memset(mrow[:].bitcast(I32), 0)
        nc.vector.memset(vrow[:].bitcast(I32), 0)
        nc.vector.memset(ths_raw[:].bitcast(I32), 0)
        make_identity(nc, ident[:])
        nc.vector.memset(xsa[:].bitcast(I32), 0)
        nc.vector.memset(dum[:], 0.0)
        nc.vector.memset(phs_raw[:].bitcast(I32), 0)
        nc.vector.memset(xsb[:].bitcast(I32), 0)
        for row, vec in ((0, gamma), (4, c)):
            nc.scalar.dma_start(
                out=vrow[row : row + 4, :].rearrange("t (a i) -> t a i", i=4),
                in_=vec.rearrange("(a t i) -> t a i", t=4, i=4),
            )
        nc.scalar.dma_start(out=vrow[8:16, :], in_=z.rearrange("(c n) -> c n", n=P))
        nc.scalar.dma_start(out=mrow[0:16, :], in_=mu.rearrange("(c n) -> c n", n=P))
        nc.scalar.activation(out=dum[:, 0:1], in_=dum[:, 1:2], func=ACTF.Sigmoid)
        load_words(th_raw, theta_words, 0, 1024)
        load_scales(ths_raw, theta_scales, 0, F, [nc.sync] * 4)
        load_words(xa, x_words, 0, 512, nc.gpsimd)
        load_scales(xsa, x_scales, 0, 256, [nc.sync] * 3 + [nc.gpsimd])
        load_words(ph_raw, phi_words, 0, 1024)
        load_scales(phs_raw, phi_scales, 0, F, [nc.sync] * 4)
        load_scales(xsb, x_scales, 256, B, [nc.gpsimd] * 4)
        load_words(xb, x_words, 512, 1024)
        load_half(0, nc.sync)
        load_words(xc, x_words, 1024, 2048)
        load_half(1, nc.sync)

        def permute_words(dst, src, g0, g1):
            nc.vector.tensor_copy(
                out=dst[:, 1024 * g0 : 1024 * g1].bitcast(I32).rearrange("p (g t a w) -> p g t a w", t=4, a=32, w=2),
                in_=src[:, 1024 * g0 : 1024 * g1].bitcast(I32).rearrange("p (g a t w) -> p g t a w", t=4, a=32, w=2),
            )

        def permute_scales(dst, src):
            nc.vector.tensor_copy(
                out=dst[:].bitcast(I32).rearrange("p (g t a) -> p g a t", t=4, a=32),
                in_=src[:].bitcast(I32).rearrange("p (g a t) -> p g a t", t=4, a=32),
            )

        def bank_tile(shape, dtype, bank):
            tile = psum.tile(shape, dtype, name="bank%d" % bank)
            return tile

        def columns(rows, n, bank):
            cps = bank_tile([P, P], BF16, bank)
            nc.tensor.transpose(cps[:], rows[:], ident[:])
            cols = keep.tile([P, n], BF16, name="cols%d" % n, align_bytes=64)
            nc.vector.tensor_copy(out=cols[:], in_=cps[:, 0:n])
            return cols

        def spread(cols, j0, bank):
            bps = bank_tile([P, 8, P], BF16, bank)
            for j in range(8):
                nc.tensor.transpose(bps[:, j, :], cols[:, j0 + j : j0 + j + 1].to_broadcast([P, P]), ident[:])
            return bps

        vcols = columns(vrow, 32, 0)
        mcols = columns(mrow, 16, 4)
        nc.vector.tensor_copy(out=gam[:], in_=vcols[:, 0:4])
        zp = spread(vcols, 8, 1)
        mu_ps = [spread(mcols, 0, 2)]
        nc.vector.scalar_tensor_tensor(out=nb[:], in0=vcols[:, 4:8], scalar=-1.0, in1=gam[:], op0=ALU.mult, op1=ALU.mult)

        def gates(tile, b0, b1):
            for t in range(T):
                nc.scalar.activation(
                    out=tile[:, t, :],
                    in_=zp[:].rearrange("p c n -> p (c n)")[:, b0:b1],
                    func=ACTF.Sigmoid,
                    bias=nb[:, t : t + 1],
                    scale=gam[:, t : t + 1],
                )

        def mu_copy():
            for h in range(2):
                nc.scalar.copy(
                    out=mub[:, 1024 * h : 1024 * (h + 1)],
                    in_=mu_ps[h][:].rearrange("p c n -> p (c n)"),
                )

        permute_words(th_w, th_raw, 0, 2)
        permute_words(th_w, th_raw, 2, 4)
        permute_scales(th_s, ths_raw)

        def x_cols(ci, g):
            b0, w = CHUNKS[ci]
            tile, first, width = (xa, 0, 256) if b0 < 256 else (xb, 256, 256) if b0 < 512 else (xc, 512, 512)
            off = 2 * (width * g + b0 - first)
            return tile[:, off : off + 2 * w]

        def x_scale_cols(ci, g):
            b0, w = CHUNKS[ci]
            tile, first, width = (xsa, 0, 256) if b0 < 256 else (xsb, 256, 768)
            off = width * g + b0 - first
            return tile[:, off : off + w]

        def stage1(ci, kind, ts, bank):
            b0, w = CHUNKS[ci]
            words, scales = (th_w, th_s) if kind == "shift" else (ph_w, ph_s)
            acc = bank_tile([P, len(ts), w], F32, bank)
            for j, t in enumerate(ts):
                for g in range(G):
                    nc.tensor.matmul_mx(
                        out=acc[:, j, :],
                        lhsT=words[:, 1024 * g + 256 * t : 1024 * g + 256 * (t + 1)].bitcast(FP4X4),
                        lhsT_scale=scales[:, F * g + P * t : F * g + P * (t + 1)],
                        rhs=x_cols(ci, g).bitcast(FP4X4),
                        rhs_scale=x_scale_cols(ci, g),
                        start=(g == 0),
                        stop=(g == G - 1),
                    )
            return acc

        gated, accs = {}, {}

        def do_shift(ci, ts):
            b0, w = CHUNKS[ci]
            acc = accs["s", ci, ts]
            tile, first = (gate_a, 0) if b0 < 256 else (gate_b, 256)
            gates_in = tile[:, ts[0] : ts[-1] + 1, b0 - first : b0 - first + w]
            if ci in ht:
                gs = tpool.tile([P, len(ts), w], F32, name="gs")
                nc.vector.tensor_tensor(out=gs[:], in0=acc[:], in1=gates_in, op=ALU.mult)
            else:
                gs = tpool.tile([P, w, len(ts)], F32, name="gs")
                nc.vector.tensor_tensor(
                    out=gs[:], in0=acc[:].rearrange("p t b -> p b t"), in1=gates_in.rearrange("p t b -> p b t"), op=ALU.mult
                )
            gated[(ci, ts[0])] = gs

        def do_base(ci, ts):
            acc = accs["b", ci, ts]
            if ci in ht:
                nc.vector.tensor_tensor(
                    out=ht[ci][:, ts[0] : ts[-1] + 1, :], in0=acc[:], in1=gated[(ci, ts[0])][:], op=ALU.add
                )
            else:
                nc.vector.tensor_tensor(
                    out=hg[ci][:, :, ts[0] : ts[-1] + 1],
                    in0=acc[:].rearrange("p t b -> p b t"),
                    in1=gated[(ci, ts[0])][:],
                    op=ALU.add,
                )

        def quant_h(ci):
            nc.vector.quantize_mx(
                out=hq[ci][:].bitcast(FP8X4), scales=hqs[ci][:], in_=hg[ci][:].rearrange("p b t -> p (b t)")
            )

        def group_load(q, engine):
            dst = lgrp[q][:].rearrange("p (n i) t -> p n t i", i=4)
            src = lraw[q // 2][:, :, NQ * (q % 2) : NQ * (q % 2 + 1)].rearrange("p t (n i) -> p n t i", i=4)
            if engine == "gpsimd":
                for n0 in (0, NQ // 8):
                    nc.gpsimd.tensor_scalar(
                        out=dst[:, n0 : n0 + NQ // 8],
                        in0=src[:, n0 : n0 + NQ // 8],
                        scalar1=1.0,
                        scalar2=0.0,
                        op0=ALU.mult,
                        op1=ALU.add,
                    )
            elif engine == "scalar":
                nc.scalar.copy(out=dst, in_=src)
            else:
                nc.vector.tensor_copy(out=dst, in_=src)

        def quant_load(q):
            nc.vector.quantize_mx(
                out=lq[q][:].bitcast(FP8X4), scales=lqs[q][:], in_=lgrp[q][:].rearrange("p d t -> p (d t)")
            )

        outs, banks, parts, done = {}, {}, {}, {}
        LATE = [(3, 0, 1), (3, 0, 0)]

        def stage2(ci, bt, q, bank):
            acc = bank_tile([P, NQ], F32, bank)
            nc.tensor.matmul_mx(
                out=acc[:],
                lhsT=hq[ci][:, P * bt : P * (bt + 1)].bitcast(FP8X4),
                lhsT_scale=hqs[ci][:, P * bt : P * (bt + 1)],
                rhs=lq[q][:].bitcast(FP8X4),
                rhs_scale=lqs[q][:],
                start=True,
                stop=True,
            )
            banks[ci, bt, q] = acc

        def out_cols(ci, bt, q):
            if (ci, bt, q // 2) not in outs:
                ob = opool.tile([P, 1024], F32, name="ob")
                outs[ci, bt, q // 2] = ob
                done[ci, bt, q // 2] = 0
            return outs[ci, bt, q // 2][:, NQ * (q % 2) : NQ * (q % 2 + 1)]

        def finished(ci, bt, q):
            key = (ci, bt, q // 2)
            done[key] += 1
            row = CHUNKS[ci][0] + P * bt
            if key in LATE:
                nc.sync.dma_start(out=out[row : row + P, NQ * q : NQ * (q + 1)], in_=out_cols(ci, bt, q))
            elif done[key] == 2:
                nc.sync.dma_start(out=out[row : row + P, 1024 * (q // 2) : 1024 * (q // 2 + 1)], in_=outs[key][:])

        def add_mu(ci, bt, q):
            nc.vector.tensor_tensor(
                out=out_cols(ci, bt, q), in0=banks[ci, bt, q][:], in1=mub[:, NQ * q : NQ * (q + 1)], op=ALU.add
            )
            finished(ci, bt, q)

        def copy_out(ci, bt, q):
            cp = cpool.tile([P, NQ], F32, name="cp")
            nc.scalar.copy(out=cp[:], in_=banks[ci, bt, q][:])
            parts[ci, bt, q] = cp

        def add_mu_copied(ci, bt, q):
            nc.gpsimd.tensor_tensor(
                out=out_cols(ci, bt, q), in0=parts[ci, bt, q][:], in1=mub[:, NQ * q : NQ * (q + 1)], op=ALU.add
            )
            finished(ci, bt, q)

        STEPS = """
        x y s0b.0 p s0a.4 u vs0b b0b.5 vs0a m b0a.6 vb0b s1a.7 vb0a g1s b1a.0 g0v s4.1 q0 l0 l1 f000.4 f010.5
        vs4 c000 f001.2 b4.3 vs1a c010 a000 e001 g2s vb1a s2b.6 a010 vb4 f011.1 vs2b s2a.4 q4 c011 l2 f400.7
        g3s vs2a a011 f401.5 f402.2 s1b.0 e400 e401 b1b.3 vs1b c402 l3 f012.6 f002.1 a402 vb1b c012 f403.4
        f003.7 e002 f013.5 h1 b2a.0 a012 e003 e403 c013 b2b.2 q1 a013 vb2a f112.3 vb2b f111.6 c112 f110.1
        f101.7 e111 f113.4 h2 a112 f102.5 e110 f103.0 f100.2 e113 s3.3 c102 q2 e103 a102 f203.6 e100 f213.1
        c203 f202.4 e101 f200.5 f201.0 a203 c200 f212.2 e202 f211.6 b3.7 c212 e201 a200 vs3 f210.5 e213 a212
        vb3 e210 q3 e211 f300.4 f303.2 e300 f301.0 c303 f302.3 e301 a303 e302
        """.split()
        SLOTS = {"a": (0, 1), "b": (2, 3)}
        for tok in STEPS:
            k = tok[0]
            if k in "sb":
                unit, bank = tok.split(".")
                ts = SLOTS.get(unit[-1], (0, 1, 2, 3))
                accs[k, int(unit[1]), ts] = stage1(int(unit[1]), "shift" if k == "s" else "base", ts, int(bank))
            elif k == "f":
                stage2(*[int(ch) for ch in tok[1:4]], bank=int(tok[5]))
            elif k == "h":
                ci = int(tok[1])
                nc.scalar.copy(
                    out=hg[ci][:].rearrange("p (n i) t -> p n t i", i=4),
                    in_=ht[ci][:].rearrange("p t (n i) -> p n t i", i=4),
                )
            elif k == "v":
                ts = SLOTS.get(tok[-1], (0, 1, 2, 3))
                (do_shift if tok[1] == "s" else do_base)(int(tok[2]), ts)
            elif k == "p":
                permute_words(ph_w, ph_raw, 0, 2)
                permute_words(ph_w, ph_raw, 2, 4)
                permute_scales(ph_s, phs_raw)
            elif k == "x":
                gates(gate_a, 0, 256)
            elif k == "y":
                gates(gate_b, 256, 1024)
            elif k == "u":
                mu_ps.append(spread(mcols, 8, 3))
            elif k == "m":
                mu_copy()
            elif k == "g":
                group_load(int(tok[1]), {"s": "scalar", "v": "vector", "g": "gpsimd"}[tok[2]])
            elif k == "l":
                quant_load(int(tok[1]))
            elif k == "q":
                quant_h(int(tok[1]))
            else:
                {"e": add_mu, "c": copy_out, "a": add_mu_copied}[k](*[int(ch) for ch in tok[1:]])
